import numpy as np
import ml_dtypes


def mxq(x, axis, fmt="e4m3"):
    dtype, down = {"e4m3": (ml_dtypes.float8_e4m3fn, 7), "e5m2": (ml_dtypes.float8_e5m2, 14)}[fmt]
    v = np.moveaxis(np.asarray(x, np.float32).astype(ml_dtypes.bfloat16).astype(np.float64), axis, -1)
    blocks = v.reshape(v.shape[:-1] + (-1, 32))
    amax = np.abs(blocks).max(-1, keepdims=True)
    byte = np.maximum(np.where(amax > 0, np.frexp(amax)[1] - 1 + 127, 0) - down, 1)
    scale = np.exp2(byte - 127.0)
    codes = (blocks / scale).astype(np.float32).astype(dtype).astype(np.float64)
    return np.moveaxis((codes * scale).reshape(v.shape), -1, axis)


WIDE = False


def mx_kscale(k):
    if not WIDE:
        return np.ones(k)
    levels = np.array([10, -10, 5, -5, 0])
    if k % 512:
        return np.exp2(np.random.permutation(np.resize(levels, k // 32))).repeat(32)
    a = np.empty((k // 512, 16))
    for p in range(k // 512):
        a[p, :8] = np.random.permutation(np.resize(levels, 8))
        for g in range(8):
            far = levels[np.abs(levels - a[p, g]) >= 10]
            a[p, g + 8] = far[np.random.randint(len(far))]
    return np.exp2(a.ravel()).repeat(32)


def f64(x):
    return np.asarray(x).astype(np.float64)


def striped(idx):
    return np.tile(np.asarray(idx).reshape(-1, 16).T, (8, 1)).astype(np.uint16)


def unstriped(offs):
    return offs[:16].T.reshape(-1).astype(np.int64)


E2M1 = np.array([0.0, 0.5, 1.0, 1.5, 2.0, 3.0, 4.0, 6.0, -0.0, -0.5, -1.0, -1.5, -2.0, -3.0, -4.0, -6.0])


def pack_weight(w, fmt):
    k, n = w.shape
    w = f64(np.asarray(w, np.float32).astype(ml_dtypes.bfloat16)).reshape(k // 32, 32, n)
    amax = np.abs(w).max(1)
    if fmt == "e4m3":
        byte = np.frexp(amax)[1] - 1 + 127 - 7
    else:
        mant, ex = np.frexp(amax / 6.0)
        byte = np.where(mant > 0.5, ex, ex - 1) + 127
    byte = np.clip(np.where(amax > 0, byte, 1), 1, 254)
    scaled = (w * np.exp2(127.0 - byte)[:, None, :]).reshape(k, n).astype(np.float32)
    by_word = np.ascontiguousarray(scaled.reshape(k // 512, 128, 4, n).transpose(0, 1, 3, 2))
    if fmt == "e4m3":
        words = by_word.astype(ml_dtypes.float8_e4m3fn).view(np.uint8)
    else:
        c = by_word.astype(ml_dtypes.float4_e2m1fn).view(np.uint8) & 0xF
        words = (c[..., 0::2] | (c[..., 1::2] << 4)).reshape(k // 512, 128, 2 * n)
    return np.ascontiguousarray(words), np.ascontiguousarray(byte.astype(np.uint8).reshape(k // 512, 16, n))


def unpack_weight(words, scales, fmt):
    g, _, n = scales.shape
    words = np.ascontiguousarray(words).reshape(g, 128, n, -1)
    if fmt == "e4m3":
        vals = words.view(ml_dtypes.float8_e4m3fn).astype(np.float64)
    else:
        nib = np.empty((g, 128, n, 4), np.uint8)
        nib[..., 0::2] = words & 0xF
        nib[..., 1::2] = words >> 4
        vals = E2M1[nib]
    vals = vals * np.repeat(np.exp2(scales.astype(np.float64) - 127.0), 8, axis=1)[..., None]
    return vals.transpose(0, 1, 3, 2).reshape(g * 512, n)


D, E, T, R, I, Q = 512, 512, 2048, 1024, 512, 128


def setup_inputs():
    n = np.random.standard_normal
    idx = np.random.permutation(T)[:R]
    idx2 = np.random.permutation(R)[:I]
    fd = mx_kscale(D)
    fe = mx_kscale(E)
    keysp = pack_weight(n((D, T)) / fd[:, None], "e2m1")
    valsp = pack_weight(n((E, T)) / fe[:, None], "e2m1")
    return {
        "query": (n((D, Q)) * 0.6 / np.sqrt(D) * fd[:, None]).astype(np.float32),
        "keys_words": keysp[0],
        "keys_scales": keysp[1],
        "gout": (n((E, Q)) * 1 / np.sqrt(E) * fe[:, None]).astype(np.float32),
        "vals_words": valsp[0],
        "vals_scales": valsp[1],
        "lse": (np.random.uniform(6.2, 6.5, (Q, 1))).astype(np.float32),
        "delta": (np.random.uniform(-0.3, 0.3, (Q, 1))).astype(np.float32),
        "old": (0.5 * n((Q, R))).astype(np.float32),
        "fade": (np.random.uniform(0.5, 1.0, (1, R))).astype(np.float32),
        "offs": striped(idx),
        "offs2": striped(idx2),
    }


def reference(query, keys_words, keys_scales, gout, vals_words, vals_scales, lse, delta, old, fade, offs, offs2):
    idx = unstriped(offs)
    idx2 = unstriped(offs2)
    keysu = unpack_weight(keys_words, keys_scales, "e2m1")
    valsu = unpack_weight(vals_words, vals_scales, "e2m1")
    queryq = mxq(f64(query), 0, "e4m3")
    keysidxg = keysu[:, idx]
    a = queryq.T @ keysidxg
    goutq = mxq(f64(gout), 0, "e4m3")
    valsidxg = valsu[:, idx]
    dp = goutq.T @ valsidxg
    ds = np.exp(a[:, idx2] - f64(lse)) * (dp[:, idx2] - f64(delta)) * 512.0
    df = np.zeros((Q, R))
    df[:, idx2] = ds
    y = f64(old) * f64(fade) + df
    return y

@@ -1,0 +1,157 @@
+from contextlib import ExitStack
+
+import concourse.mybir as mybir
+from concourse.masks import make_identity
+
+D, T, R, I, Q = 512, 2048, 1024, 512, 128
+FLOPS = 2 * 2 * D * Q * R
+
+F32 = mybir.dt.float32
+BF16 = mybir.dt.bfloat16
+I32 = mybir.dt.int32
+U32 = mybir.dt.uint32
+U16 = mybir.dt.uint16
+U8 = mybir.dt.uint8
+FP8X4 = mybir.dt.float8_e4m3fn_x4
+FP4X4 = mybir.dt.float4_e2m1fn_x4
+ACT = mybir.ActivationFunctionType
+ALU = mybir.AluOpType
+
+P = 128
+PACK = 4
+BANK = 512
+GAIN = 512.0
+STORE = 256
+STEP_PIECES = ((0, 256), (256, 512))
+KEY_PIECES = ((0, 512), (512, 1024))
+VAL_PIECES = ((0, 512), (512, 768), (768, 1024))
+
+
+def tile_attend_gresident_kernel(tc, query, keys_words, keys_scales, gout, vals_words, vals_scales,
+                                  lse, delta, old, fade, offs, offs2, out):
+    nc = tc.nc
+    with ExitStack() as ctx:
+        lists = ctx.enter_context(tc.tile_pool(name="lists", bufs=1))
+        sb = ctx.enter_context(tc.tile_pool(name="sb", bufs=1))
+        psum = ctx.enter_context(tc.psum_pool(name="psum", bufs=1))
+
+        resident = lists.tile([P, R // 16], U16, name="resident")
+        picked = lists.tile([P, I // 16], U16, name="picked")
+
+        key_bytes = sb.tile([P, T], U8, name="key_bytes", align_bytes=64)
+        val_bytes = sb.tile([P, T], U8, name="val_bytes", align_bytes=64)
+        key_words = sb.tile([P, T], U16, name="key_words", align_bytes=64)
+        val_words = sb.tile([P, T], U16, name="val_words", tag="val_pool", align_bytes=64)
+        df = sb.tile([P, R], F32, name="df", align_bytes=64)
+
+        nc.vector.memset(key_bytes[:].bitcast(I32), 0)
+        nc.vector.memset(val_bytes[:].bitcast(I32), 0)
+        nc.vector.memset(df[:], 0.0)
+
+        def load_scale_rows(dst, src):
+            for quad in range(4):
+                nc.sync.dma_start(out=dst[32 * quad : 32 * quad + 4, :].bitcast(I32),
+                                  in_=src[0, 4 * quad : 4 * quad + 4, :].bitcast(I32))
+
+        q_raw = sb.tile([P, PACK, Q], F32, name="q_raw")
+        g_raw = sb.tile([P, PACK, Q], F32, name="g_raw")
+        lse_col = sb.tile([P, 1], F32, name="lse_col")
+        delta_col = sb.tile([P, 1], F32, name="delta_col")
+        old_sb = sb.tile([P, R], F32, name="old_sb")
+        fade_cols = sb.tile([P, R // P], F32, name="fade_cols")
+
+        nc.sync.dma_start(resident[:], offs)
+        nc.sync.dma_start(out=key_words[:].bitcast(I32), in_=keys_words[0].bitcast(I32))
+        load_scale_rows(key_bytes, keys_scales)
+        nc.sync.dma_start(out=q_raw[:], in_=query.rearrange("(p j) w -> p j w", j=PACK))
+        nc.sync.dma_start(out=g_raw[:], in_=gout.rearrange("(p j) w -> p j w", j=PACK))
+        load_scale_rows(val_bytes, vals_scales)
+        nc.sync.dma_start(out=val_words[:].bitcast(I32), in_=vals_words[0].bitcast(I32))
+        nc.sync.dma_start(picked[:], offs2)
+        nc.sync.dma_start(out=lse_col[:], in_=lse)
+        nc.sync.dma_start(out=delta_col[:], in_=delta)
+        nc.sync.dma_start(out=old_sb[:], in_=old)
+        with nc.allow_non_contiguous_dma(reason="one fading factor to a partition and chunk"):
+            nc.sync.dma_start(out=fade_cols[:], in_=fade.rearrange("o (c p) -> p (o c)", p=P))
+
+        ident = sb.tile([P, P], F32, name="ident")
+        make_identity(nc, ident[:])
+
+        def gather_words(pool_words, pieces, label):
+            tiles = []
+            for lo, hi in pieces:
+                piece = sb.tile([P, hi - lo], U16, name="%s_words_%d" % (label, lo), align_bytes=64)
+                nc.vector.tensor_copy(piece[:], pool_words[:].indirect(resident[:, lo // 16 : hi // 16]))
+                tiles.append(piece)
+            return tiles
+
+        def gather_bytes(pool_bytes, label):
+            listed = sb.tile([P, R], U8, name="%s_bytes_listed" % label, align_bytes=64)
+            nc.vector.tensor_copy(listed[:], pool_bytes[:].indirect(resident[:]))
+            return listed
+
+        def product(which, pieces, words, scale_bytes, result, label):
+            cols = slice(which * Q, (which + 1) * Q)
+            for (lo, hi), piece in zip(pieces, words):
+                bank = psum.tile([P, hi - lo], F32, name="%s_bank_%d" % (label, lo))
+                nc.tensor.matmul_mx(out=bank[:], lhsT=codes[:, cols].bitcast(FP8X4), lhsT_scale=scales[:, cols],
+                                    rhs=piece[:].bitcast(FP4X4), rhs_scale=scale_bytes[:, lo:hi],
+                                    start=True, stop=True)
+                nc.scalar.copy(out=result[:, lo:hi], in_=bank[:])
+
+        k_words = gather_words(key_words, KEY_PIECES, "k")
+        k_bytes = gather_bytes(key_bytes, "k")
+
+        grouped = sb.tile([P, 2 * Q, PACK], BF16, name="grouped", align_bytes=64)
+        nc.scalar.copy(out=grouped[:, 0:Q, :], in_=q_raw[:].rearrange("p j w -> p w j"))
+        nc.scalar.copy(out=grouped[:, Q : 2 * Q, :], in_=g_raw[:].rearrange("p j w -> p w j"))
+        codes = sb.tile([P, 2 * Q], U32, name="codes", align_bytes=64)
+        scales = sb.tile([P, 2 * Q], U8, name="scales", align_bytes=64)
+        nc.vector.quantize_mx(out=codes[:].bitcast(FP8X4), scales=scales[:],
+                              in_=grouped[:].rearrange("p w j -> p (w j)"))
+
+        a_sb = sb.tile([P, R], F32, name="a_sb")
+        product(0, KEY_PIECES, k_words, k_bytes, a_sb, "a")
+
+        v_bytes = gather_bytes(val_bytes, "v")
+        v_words = gather_words(val_words, VAL_PIECES, "v")
+        dp_sb = sb.tile([P, R], F32, name="dp_sb")
+        product(1, VAL_PIECES, v_words, v_bytes, dp_sb, "dp")
+
+        neg_lse = sb.tile([P, 1], F32, name="neg_lse")
+        nc.scalar.activation(out=neg_lse[:], in_=lse_col[:], func=ACT.Copy, scale=-1.0)
+        neg_delta = sb.tile([P, 1], F32, name="neg_delta")
+        nc.scalar.activation(out=neg_delta[:], in_=delta_col[:], func=ACT.Copy, scale=-GAIN)
+
+        a_picked = sb.tile([P, I], F32, name="a_picked", tag="val_pool", align_bytes=64)
+        nc.vector.tensor_copy(a_picked[:], a_sb[:].indirect(picked[:]))
+        weights = sb.tile([P, I], F32, name="weights")
+        nc.scalar.activation(out=weights[:], in_=a_picked[:], func=ACT.Exp, bias=neg_lse[:], scale=1.0)
+        centred = []
+        for lo, hi in STEP_PIECES:
+            dp_picked = sb.tile([P, hi - lo], F32, name="dp_picked_%d" % lo)
+            nc.vector.tensor_copy(dp_picked[:], dp_sb[:].indirect(picked[:, lo // 16 : hi // 16]))
+            piece = sb.tile([P, hi - lo], F32, name="centred_%d" % lo)
+            nc.scalar.activation(out=piece[:], in_=dp_picked[:], func=ACT.Identity, bias=neg_delta[:], scale=GAIN)
+            centred.append(piece)
+        for (lo, hi), piece in zip(STEP_PIECES, centred):
+            nc.vector.tensor_tensor(df[:].indirect(picked[:, lo // 16 : hi // 16]), piece[:], weights[:, lo:hi], ALU.mult)
+
+        for half in range(R // BANK):
+            turned = psum.tile([P, BANK], F32, name="turned")
+            faded_t = sb.tile([P, BANK], F32, name="faded_t_%d" % half)
+            faded = psum.tile([P, BANK], F32, name="faded_%d" % half)
+            for c in range(BANK // P):
+                r0 = half * BANK + c * P
+                nc.tensor.transpose(turned[:, c * P : (c + 1) * P], old_sb[:, r0 : r0 + P], ident[:])
+            for c in range(BANK // P):
+                chunk = half * (BANK // P) + c
+                nc.scalar.activation(out=faded_t[:, c * P : (c + 1) * P], in_=turned[:, c * P : (c + 1) * P],
+                                     func=ACT.Copy, scale=fade_cols[:, chunk : chunk + 1])
+            for c in range(BANK // P):
+                nc.tensor.transpose(faded[:, c * P : (c + 1) * P], faded_t[:, c * P : (c + 1) * P], ident[:])
+            for lo in range(0, BANK, STORE):
+                result = sb.tile([P, STORE], F32, name="result_%d_%d" % (half, lo))
+                cols = slice(half * BANK + lo, half * BANK + lo + STORE)
+                nc.vector.tensor_tensor(result[:], df[:, cols], faded[:, lo : lo + STORE], ALU.add)
+                nc.sync.dma_start(out=out[:, cols], in_=result[:])

@@ -66,13 +66,13 @@ def tile_attend_gresident_kernel(tc, query, keys_words, keys_scales, gout, vals_
         nc.sync.dma_start(out=q_raw[:], in_=query.rearrange("(p j) w -> p j w", j=PACK))
         nc.sync.dma_start(out=g_raw[:], in_=gout.rearrange("(p j) w -> p j w", j=PACK))
         load_scale_rows(val_bytes, vals_scales)
+        nc.sync.dma_start(out=old_sb[:], in_=old)
+        with nc.allow_non_contiguous_dma(reason="one fading factor to a partition and chunk"):
+            nc.sync.dma_start(out=fade_cols[:], in_=fade.rearrange("o (c p) -> p (o c)", p=P))
         nc.sync.dma_start(out=val_words[:].bitcast(I32), in_=vals_words[0].bitcast(I32))
         nc.sync.dma_start(picked[:], offs2)
         nc.sync.dma_start(out=lse_col[:], in_=lse)
         nc.sync.dma_start(out=delta_col[:], in_=delta)
-        nc.sync.dma_start(out=old_sb[:], in_=old)
-        with nc.allow_non_contiguous_dma(reason="one fading factor to a partition and chunk"):
-            nc.sync.dma_start(out=fade_cols[:], in_=fade.rearrange("o (c p) -> p (o c)", p=P))
 
         ident = sb.tile([P, P], F32, name="ident")
         make_identity(nc, ident[:])
@@ -93,7 +93,7 @@ def tile_attend_gresident_kernel(tc, query, keys_words, keys_scales, gout, vals_
         def product(which, pieces, words, scale_bytes, result, label):
             cols = slice(which * Q, (which + 1) * Q)
             for (lo, hi), piece in zip(pieces, words):
-                bank = psum.tile([P, hi - lo], F32, name="%s_bank_%d" % (label, lo))
+                bank = psum.tile([P, hi - lo], F32, name="%s_bank_%d" % (label, lo), tag="%s_bank_%d" % (label, lo))
                 nc.tensor.matmul_mx(out=bank[:], lhsT=codes[:, cols].bitcast(FP8X4), lhsT_scale=scales[:, cols],
                                     rhs=piece[:].bitcast(FP4X4), rhs_scale=scale_bytes[:, lo:hi],
                                     start=True, stop=True)
@@ -112,6 +112,22 @@ def tile_attend_gresident_kernel(tc, query, keys_words, keys_scales, gout, vals_
 
         a_sb = sb.tile([P, R], F32, name="a_sb")
         product(0, KEY_PIECES, k_words, k_bytes, a_sb, "a")
+
+        faded_halves = []
+        for half in range(R // BANK):
+            turned = psum.tile([P, BANK], F32, name="turned_%d" % half, tag="dp_bank_%d" % VAL_PIECES[half + 1][0])
+            faded_t = sb.tile([P, BANK], F32, name="faded_t_%d" % half)
+            faded = psum.tile([P, BANK], F32, name="faded_%d" % half)
+            for c in range(BANK // P):
+                r0 = half * BANK + c * P
+                nc.tensor.transpose(turned[:, c * P : (c + 1) * P], old_sb[:, r0 : r0 + P], ident[:])
+            for c in range(BANK // P):
+                chunk = half * (BANK // P) + c
+                nc.scalar.activation(out=faded_t[:, c * P : (c + 1) * P], in_=turned[:, c * P : (c + 1) * P],
+                                     func=ACT.Copy, scale=fade_cols[:, chunk : chunk + 1])
+            for c in range(BANK // P):
+                nc.tensor.transpose(faded[:, c * P : (c + 1) * P], faded_t[:, c * P : (c + 1) * P], ident[:])
+            faded_halves.append(faded)
 
         v_bytes = gather_bytes(val_bytes, "v")
         v_words = gather_words(val_words, VAL_PIECES, "v")
@@ -138,20 +154,8 @@ def tile_attend_gresident_kernel(tc, query, keys_words, keys_scales, gout, vals_
             nc.vector.tensor_tensor(df[:].indirect(picked[:, lo // 16 : hi // 16]), piece[:], weights[:, lo:hi], ALU.mult)
 
         for half in range(R // BANK):
-            turned = psum.tile([P, BANK], F32, name="turned")
-            faded_t = sb.tile([P, BANK], F32, name="faded_t_%d" % half)
-            faded = psum.tile([P, BANK], F32, name="faded_%d" % half)
-            for c in range(BANK // P):
-                r0 = half * BANK + c * P
-                nc.tensor.transpose(turned[:, c * P : (c + 1) * P], old_sb[:, r0 : r0 + P], ident[:])
-            for c in range(BANK // P):
-                chunk = half * (BANK // P) + c
-                nc.scalar.activation(out=faded_t[:, c * P : (c + 1) * P], in_=turned[:, c * P : (c + 1) * P],
-                                     func=ACT.Copy, scale=fade_cols[:, chunk : chunk + 1])
-            for c in range(BANK // P):
-                nc.tensor.transpose(faded[:, c * P : (c + 1) * P], faded_t[:, c * P : (c + 1) * P], ident[:])
             for lo in range(0, BANK, STORE):
                 result = sb.tile([P, STORE], F32, name="result_%d_%d" % (half, lo))
                 cols = slice(half * BANK + lo, half * BANK + lo + STORE)
-                nc.vector.tensor_tensor(result[:], df[:, cols], faded[:, lo : lo + STORE], ALU.add)
+                nc.vector.tensor_tensor(result[:], df[:, cols], faded_halves[half][:, lo : lo + STORE], ALU.add)
                 nc.sync.dma_start(out=out[:, cols], in_=result[:])

@@ -22,7 +22,7 @@ PACK = 4
 BANK = 512
 GAIN = 512.0
 STORE = 256
-STEP_PIECES = ((0, 256), (256, 512))
+STEP_PIECES = ((0, 192), (192, 512))
 KEY_PIECES = ((0, 512), (512, 1024))
 VAL_PIECES = ((0, 512), (512, 768), (768, 1024))
 
@@ -46,6 +46,8 @@ def tile_attend_gresident_kernel(tc, query, keys_words, keys_scales, gout, vals_
 
         nc.vector.memset(key_bytes[:].bitcast(I32), 0)
         nc.vector.memset(val_bytes[:].bitcast(I32), 0)
+        fade_rows = sb.tile([P, P], F32, name="fade_rows")
+        nc.vector.memset(fade_rows[:], 0.0)
         nc.vector.memset(df[:], 0.0)
 
         def load_scale_rows(dst, src):
@@ -67,8 +69,7 @@ def tile_attend_gresident_kernel(tc, query, keys_words, keys_scales, gout, vals_
         nc.sync.dma_start(out=g_raw[:], in_=gout.rearrange("(p j) w -> p j w", j=PACK))
         load_scale_rows(val_bytes, vals_scales)
         nc.sync.dma_start(out=old_sb[:], in_=old)
-        with nc.allow_non_contiguous_dma(reason="one fading factor to a partition and chunk"):
-            nc.sync.dma_start(out=fade_cols[:], in_=fade.rearrange("o (c p) -> p (o c)", p=P))
+        nc.sync.dma_start(out=fade_rows[0 : R // P, :], in_=fade.rearrange("o (c p) -> (o c) p", p=P))
         nc.sync.dma_start(out=val_words[:].bitcast(I32), in_=vals_words[0].bitcast(I32))
         nc.sync.dma_start(picked[:], offs2)
         nc.sync.dma_start(out=lse_col[:], in_=lse)
@@ -113,6 +114,9 @@ def tile_attend_gresident_kernel(tc, query, keys_words, keys_scales, gout, vals_
         a_sb = sb.tile([P, R], F32, name="a_sb")
         product(0, KEY_PIECES, k_words, k_bytes, a_sb, "a")
 
+        fade_turned = psum.tile([P, P], F32, name="fade_turned")
+        nc.tensor.transpose(fade_turned[:], fade_rows[:], ident[:])
+        nc.scalar.copy(out=fade_cols[:], in_=fade_turned[:, 0 : R // P])
         faded_halves = []
         for half in range(R // BANK):
             turned = psum.tile([P, BANK], F32, name="turned_%d" % half, tag="dp_bank_%d" % VAL_PIECES[half + 1][0])
@@ -142,9 +146,9 @@ def tile_attend_gresident_kernel(tc, query, keys_words, keys_scales, gout, vals_
         a_picked = sb.tile([P, I], F32, name="a_picked", tag="val_pool", align_bytes=64)
         nc.vector.tensor_copy(a_picked[:], a_sb[:].indirect(picked[:]))
         weights = sb.tile([P, I], F32, name="weights")
-        nc.scalar.activation(out=weights[:], in_=a_picked[:], func=ACT.Exp, bias=neg_lse[:], scale=1.0)
         centred = []
         for lo, hi in STEP_PIECES:
+            nc.scalar.activation(out=weights[:, lo:hi], in_=a_picked[:, lo:hi], func=ACT.Exp, bias=neg_lse[:], scale=1.0)
             dp_picked = sb.tile([P, hi - lo], F32, name="dp_picked_%d" % lo)
             nc.vector.tensor_copy(dp_picked[:], dp_sb[:].indirect(picked[:, lo // 16 : hi // 16]))
             piece = sb.tile([P, hi - lo], F32, name="centred_%d" % lo)

@@ -22,7 +22,7 @@ PACK = 4
 BANK = 512
 GAIN = 512.0
 STORE = 256
-STEP_PIECES = ((0, 192), (192, 512))
+STEP_PIECES = ((0, 256), (256, 512))
 KEY_PIECES = ((0, 512), (512, 1024))
 VAL_PIECES = ((0, 512), (512, 768), (768, 1024))
 
@@ -39,9 +39,9 @@ def tile_attend_gresident_kernel(tc, query, keys_words, keys_scales, gout, vals_
         picked = lists.tile([P, I // 16], U16, name="picked")
 
         key_bytes = sb.tile([P, T], U8, name="key_bytes", align_bytes=64)
-        val_bytes = sb.tile([P, T], U8, name="val_bytes", align_bytes=64)
+        val_bytes = sb.tile([P, T], U8, name="val_bytes", tag="val_pool", align_bytes=64)
         key_words = sb.tile([P, T], U16, name="key_words", align_bytes=64)
-        val_words = sb.tile([P, T], U16, name="val_words", tag="val_pool", align_bytes=64)
+        val_words = sb.tile([P, T], U16, name="val_words", align_bytes=64)
         df = sb.tile([P, R], F32, name="df", align_bytes=64)
 
         nc.vector.memset(key_bytes[:].bitcast(I32), 0)
@@ -64,13 +64,13 @@ def tile_attend_gresident_kernel(tc, query, keys_words, keys_scales, gout, vals_
 
         nc.sync.dma_start(resident[:], offs)
         nc.sync.dma_start(out=key_words[:].bitcast(I32), in_=keys_words[0].bitcast(I32))
+        nc.sync.dma_start(out=val_words[:].bitcast(I32), in_=vals_words[0].bitcast(I32))
         load_scale_rows(key_bytes, keys_scales)
         nc.sync.dma_start(out=q_raw[:], in_=query.rearrange("(p j) w -> p j w", j=PACK))
         nc.sync.dma_start(out=g_raw[:], in_=gout.rearrange("(p j) w -> p j w", j=PACK))
-        load_scale_rows(val_bytes, vals_scales)
         nc.sync.dma_start(out=old_sb[:], in_=old)
         nc.sync.dma_start(out=fade_rows[0 : R // P, :], in_=fade.rearrange("o (c p) -> (o c) p", p=P))
-        nc.sync.dma_start(out=val_words[:].bitcast(I32), in_=vals_words[0].bitcast(I32))
+        load_scale_rows(val_bytes, vals_scales)
         nc.sync.dma_start(picked[:], offs2)
         nc.sync.dma_start(out=lse_col[:], in_=lse)
         nc.sync.dma_start(out=delta_col[:], in_=delta)
@@ -78,30 +78,24 @@ def tile_attend_gresident_kernel(tc, query, keys_words, keys_scales, gout, vals_
         ident = sb.tile([P, P], F32, name="ident")
         make_identity(nc, ident[:])
 
-        def gather_words(pool_words, pieces, label):
-            tiles = []
+        def gather(pool_tile, dtype, pieces, label):
+            listed = sb.tile([P, R], dtype, name=label, align_bytes=64)
             for lo, hi in pieces:
-                piece = sb.tile([P, hi - lo], U16, name="%s_words_%d" % (label, lo), align_bytes=64)
-                nc.vector.tensor_copy(piece[:], pool_words[:].indirect(resident[:, lo // 16 : hi // 16]))
-                tiles.append(piece)
-            return tiles
-
-        def gather_bytes(pool_bytes, label):
-            listed = sb.tile([P, R], U8, name="%s_bytes_listed" % label, align_bytes=64)
-            nc.vector.tensor_copy(listed[:], pool_bytes[:].indirect(resident[:]))
+                nc.vector.tensor_copy(listed[:, lo:hi], pool_tile[:].indirect(resident[:, lo // 16 : hi // 16]))
             return listed
 
         def product(which, pieces, words, scale_bytes, result, label):
             cols = slice(which * Q, (which + 1) * Q)
-            for (lo, hi), piece in zip(pieces, words):
+            for lo, hi in pieces:
                 bank = psum.tile([P, hi - lo], F32, name="%s_bank_%d" % (label, lo), tag="%s_bank_%d" % (label, lo))
                 nc.tensor.matmul_mx(out=bank[:], lhsT=codes[:, cols].bitcast(FP8X4), lhsT_scale=scales[:, cols],
-                                    rhs=piece[:].bitcast(FP4X4), rhs_scale=scale_bytes[:, lo:hi],
+                                    rhs=words[:, lo:hi].bitcast(FP4X4), rhs_scale=scale_bytes[:, lo:hi],
                                     start=True, stop=True)
                 nc.scalar.copy(out=result[:, lo:hi], in_=bank[:])
 
-        k_words = gather_words(key_words, KEY_PIECES, "k")
-        k_bytes = gather_bytes(key_bytes, "k")
+        k_words = gather(key_words, U16, KEY_PIECES, "k_words")
+        v_words = gather(val_words, U16, KEY_PIECES, "v_words")
+        k_bytes = gather(key_bytes, U8, ((0, R),), "k_bytes")
 
         grouped = sb.tile([P, 2 * Q, PACK], BF16, name="grouped", align_bytes=64)
         nc.scalar.copy(out=grouped[:, 0:Q, :], in_=q_raw[:].rearrange("p j w -> p w j"))
@@ -111,15 +105,12 @@ def tile_attend_gresident_kernel(tc, query, keys_words, keys_scales, gout, vals_
         nc.vector.quantize_mx(out=codes[:].bitcast(FP8X4), scales=scales[:],
                               in_=grouped[:].rearrange("p w j -> p (w j)"))
 
-        a_sb = sb.tile([P, R], F32, name="a_sb")
-        product(0, KEY_PIECES, k_words, k_bytes, a_sb, "a")
-
         fade_turned = psum.tile([P, P], F32, name="fade_turned")
         nc.tensor.transpose(fade_turned[:], fade_rows[:], ident[:])
         nc.scalar.copy(out=fade_cols[:], in_=fade_turned[:, 0 : R // P])
         faded_halves = []
         for half in range(R // BANK):
-            turned = psum.tile([P, BANK], F32, name="turned_%d" % half, tag="dp_bank_%d" % VAL_PIECES[half + 1][0])
+            turned = psum.tile([P, BANK], F32, name="turned_%d" % half, tag="a_bank_%d" % KEY_PIECES[half][0])
             faded_t = sb.tile([P, BANK], F32, name="faded_t_%d" % half)
             faded = psum.tile([P, BANK], F32, name="faded_%d" % half)
             for c in range(BANK // P):
@@ -133,8 +124,13 @@ def tile_attend_gresident_kernel(tc, query, keys_words, keys_scales, gout, vals_
                 nc.tensor.transpose(faded[:, c * P : (c + 1) * P], faded_t[:, c * P : (c + 1) * P], ident[:])
             faded_halves.append(faded)
 
-        v_bytes = gather_bytes(val_bytes, "v")
-        v_words = gather_words(val_words, VAL_PIECES, "v")
+        faded_last = sb.tile([P, STORE], F32, name="faded_last")
+        nc.scalar.copy(out=faded_last[:], in_=faded_halves[-1][:, BANK - STORE : BANK])
+
+        a_sb = sb.tile([P, R], F32, name="a_sb")
+        product(0, KEY_PIECES, k_words, k_bytes, a_sb, "a")
+
+        v_bytes = gather(val_bytes, U8, VAL_PIECES, "v_bytes")
         dp_sb = sb.tile([P, R], F32, name="dp_sb")
         product(1, VAL_PIECES, v_words, v_bytes, dp_sb, "dp")
 
@@ -157,9 +153,12 @@ def tile_attend_gresident_kernel(tc, query, keys_words, keys_scales, gout, vals_
         for (lo, hi), piece in zip(STEP_PIECES, centred):
             nc.vector.tensor_tensor(df[:].indirect(picked[:, lo // 16 : hi // 16]), piece[:], weights[:, lo:hi], ALU.mult)
 
-        for half in range(R // BANK):
-            for lo in range(0, BANK, STORE):
-                result = sb.tile([P, STORE], F32, name="result_%d_%d" % (half, lo))
-                cols = slice(half * BANK + lo, half * BANK + lo + STORE)
-                nc.vector.tensor_tensor(result[:], df[:, cols], faded_halves[half][:, lo : lo + STORE], ALU.add)
-                nc.sync.dma_start(out=out[:, cols], in_=result[:])
+        last = slice(R - STORE, R)
+        result_last = sb.tile([P, STORE], F32, name="result_last")
+        nc.gpsimd.tensor_tensor(result_last[:], df[:, last], faded_last[:], ALU.add)
+        nc.scalar.dma_start(out=out[:, last], in_=result_last[:])
+        for lo in range(0, R - STORE, STORE):
+            result = sb.tile([P, STORE], F32, name="result_%d" % lo)
+            in_bank = slice(lo % BANK, lo % BANK + STORE)
+            nc.vector.tensor_tensor(result[:], df[:, lo : lo + STORE], faded_halves[lo // BANK][:, in_bank], ALU.add)
+            nc.sync.dma_start(out=out[:, lo : lo + STORE], in_=result[:])

from contextlib import ExitStack

import concourse.mybir as mybir
from concourse.masks import make_identity

D, T, R, I, Q = 512, 2048, 1024, 512, 128
FLOPS = 2 * 2 * D * Q * R

F32 = mybir.dt.float32
BF16 = mybir.dt.bfloat16
I32 = mybir.dt.int32
U32 = mybir.dt.uint32
U16 = mybir.dt.uint16
U8 = mybir.dt.uint8
FP8X4 = mybir.dt.float8_e4m3fn_x4
FP4X4 = mybir.dt.float4_e2m1fn_x4
ACT = mybir.ActivationFunctionType
ALU = mybir.AluOpType

P = 128
PACK = 4
BANK = 512
GAIN = 512.0
STORE = 256
STEP_PIECES = ((0, 256), (256, 512))
KEY_PIECES = ((0, 512), (512, 1024))
VAL_PIECES = ((0, 512), (512, 768), (768, 1024))


def tile_attend_gresident_kernel(tc, query, keys_words, keys_scales, gout, vals_words, vals_scales,
                                  lse, delta, old, fade, offs, offs2, out):
    nc = tc.nc
    with ExitStack() as ctx:
        lists = ctx.enter_context(tc.tile_pool(name="lists", bufs=1))
        sb = ctx.enter_context(tc.tile_pool(name="sb", bufs=1))
        psum = ctx.enter_context(tc.psum_pool(name="psum", bufs=1))

        resident = lists.tile([P, R // 16], U16, name="resident")
        picked = lists.tile([P, I // 16], U16, name="picked")

        key_bytes = sb.tile([P, T], U8, name="key_bytes", align_bytes=64)
        val_bytes = sb.tile([P, T], U8, name="val_bytes", tag="val_pool", align_bytes=64)
        key_words = sb.tile([P, T], U16, name="key_words", align_bytes=64)
        val_words = sb.tile([P, T], U16, name="val_words", align_bytes=64)
        df = sb.tile([P, R], F32, name="df", align_bytes=64)

        nc.vector.memset(key_bytes[:].bitcast(I32), 0)
        nc.vector.memset(val_bytes[:].bitcast(I32), 0)
        fade_rows = sb.tile([P, P], F32, name="fade_rows")
        nc.vector.memset(fade_rows[:], 0.0)
        nc.vector.memset(df[:], 0.0)

        def load_scale_rows(dst, src):
            for quad in range(4):
                nc.sync.dma_start(out=dst[32 * quad : 32 * quad + 4, :].bitcast(I32),
                                  in_=src[0, 4 * quad : 4 * quad + 4, :].bitcast(I32))

        q_raw = sb.tile([P, PACK, Q], F32, name="q_raw")
        g_raw = sb.tile([P, PACK, Q], F32, name="g_raw")
        lse_col = sb.tile([P, 1], F32, name="lse_col")
        delta_col = sb.tile([P, 1], F32, name="delta_col")
        old_sb = sb.tile([P, R], F32, name="old_sb")
        fade_cols = sb.tile([P, R // P], F32, name="fade_cols")

        nc.sync.dma_start(resident[:], offs)
        nc.sync.dma_start(out=key_words[:].bitcast(I32), in_=keys_words[0].bitcast(I32))
        nc.sync.dma_start(out=val_words[:].bitcast(I32), in_=vals_words[0].bitcast(I32))
        load_scale_rows(key_bytes, keys_scales)
        nc.sync.dma_start(out=q_raw[:], in_=query.rearrange("(p j) w -> p j w", j=PACK))
        nc.sync.dma_start(out=g_raw[:], in_=gout.rearrange("(p j) w -> p j w", j=PACK))
        nc.sync.dma_start(out=old_sb[:], in_=old)
        nc.sync.dma_start(out=fade_rows[0 : R // P, :], in_=fade.rearrange("o (c p) -> (o c) p", p=P))
        load_scale_rows(val_bytes, vals_scales)
        nc.sync.dma_start(picked[:], offs2)
        nc.sync.dma_start(out=lse_col[:], in_=lse)
        nc.sync.dma_start(out=delta_col[:], in_=delta)

        ident = sb.tile([P, P], F32, name="ident")
        make_identity(nc, ident[:])

        def gather(pool_tile, dtype, pieces, label):
            listed = sb.tile([P, R], dtype, name=label, align_bytes=64)
            for lo, hi in pieces:
                nc.vector.tensor_copy(listed[:, lo:hi], pool_tile[:].indirect(resident[:, lo // 16 : hi // 16]))
            return listed

        def product(which, pieces, words, scale_bytes, result, label):
            cols = slice(which * Q, (which + 1) * Q)
            for lo, hi in pieces:
                bank = psum.tile([P, hi - lo], F32, name="%s_bank_%d" % (label, lo), tag="%s_bank_%d" % (label, lo))
                nc.tensor.matmul_mx(out=bank[:], lhsT=codes[:, cols].bitcast(FP8X4), lhsT_scale=scales[:, cols],
                                    rhs=words[:, lo:hi].bitcast(FP4X4), rhs_scale=scale_bytes[:, lo:hi],
                                    start=True, stop=True)
                nc.scalar.copy(out=result[:, lo:hi], in_=bank[:])

        k_words = gather(key_words, U16, KEY_PIECES, "k_words")
        v_words = gather(val_words, U16, KEY_PIECES, "v_words")
        k_bytes = gather(key_bytes, U8, ((0, R),), "k_bytes")

        grouped = sb.tile([P, 2 * Q, PACK], BF16, name="grouped", align_bytes=64)
        nc.scalar.copy(out=grouped[:, 0:Q, :], in_=q_raw[:].rearrange("p j w -> p w j"))
        nc.scalar.copy(out=grouped[:, Q : 2 * Q, :], in_=g_raw[:].rearrange("p j w -> p w j"))
        codes = sb.tile([P, 2 * Q], U32, name="codes", align_bytes=64)
        scales = sb.tile([P, 2 * Q], U8, name="scales", align_bytes=64)
        nc.vector.quantize_mx(out=codes[:].bitcast(FP8X4), scales=scales[:],
                              in_=grouped[:].rearrange("p w j -> p (w j)"))

        fade_turned = psum.tile([P, P], F32, name="fade_turned")
        nc.tensor.transpose(fade_turned[:], fade_rows[:], ident[:])
        nc.scalar.copy(out=fade_cols[:], in_=fade_turned[:, 0 : R // P])
        faded_halves = []
        for half in range(R // BANK):
            turned = psum.tile([P, BANK], F32, name="turned_%d" % half, tag="a_bank_%d" % KEY_PIECES[half][0])
            faded_t = sb.tile([P, BANK], F32, name="faded_t_%d" % half)
            faded = psum.tile([P, BANK], F32, name="faded_%d" % half)
            for c in range(BANK // P):
                r0 = half * BANK + c * P
                nc.tensor.transpose(turned[:, c * P : (c + 1) * P], old_sb[:, r0 : r0 + P], ident[:])
            for c in range(BANK // P):
                chunk = half * (BANK // P) + c
                nc.scalar.activation(out=faded_t[:, c * P : (c + 1) * P], in_=turned[:, c * P : (c + 1) * P],
                                     func=ACT.Copy, scale=fade_cols[:, chunk : chunk + 1])
            for c in range(BANK // P):
                nc.tensor.transpose(faded[:, c * P : (c + 1) * P], faded_t[:, c * P : (c + 1) * P], ident[:])
            faded_halves.append(faded)

        faded_last = sb.tile([P, STORE], F32, name="faded_last")
        nc.scalar.copy(out=faded_last[:], in_=faded_halves[-1][:, BANK - STORE : BANK])

        a_sb = sb.tile([P, R], F32, name="a_sb")
        product(0, KEY_PIECES, k_words, k_bytes, a_sb, "a")

        v_bytes = gather(val_bytes, U8, VAL_PIECES, "v_bytes")
        dp_sb = sb.tile([P, R], F32, name="dp_sb")
        product(1, VAL_PIECES, v_words, v_bytes, dp_sb, "dp")

        neg_lse = sb.tile([P, 1], F32, name="neg_lse")
        nc.scalar.activation(out=neg_lse[:], in_=lse_col[:], func=ACT.Copy, scale=-1.0)
        neg_delta = sb.tile([P, 1], F32, name="neg_delta")
        nc.scalar.activation(out=neg_delta[:], in_=delta_col[:], func=ACT.Copy, scale=-GAIN)

        a_picked = sb.tile([P, I], F32, name="a_picked", tag="val_pool", align_bytes=64)
        nc.vector.tensor_copy(a_picked[:], a_sb[:].indirect(picked[:]))
        weights = sb.tile([P, I], F32, name="weights")
        centred = []
        for lo, hi in STEP_PIECES:
            nc.scalar.activation(out=weights[:, lo:hi], in_=a_picked[:, lo:hi], func=ACT.Exp, bias=neg_lse[:], scale=1.0)
            dp_picked = sb.tile([P, hi - lo], F32, name="dp_picked_%d" % lo)
            nc.vector.tensor_copy(dp_picked[:], dp_sb[:].indirect(picked[:, lo // 16 : hi // 16]))
            piece = sb.tile([P, hi - lo], F32, name="centred_%d" % lo)
            nc.scalar.activation(out=piece[:], in_=dp_picked[:], func=ACT.Identity, bias=neg_delta[:], scale=GAIN)
            centred.append(piece)
        for (lo, hi), piece in zip(STEP_PIECES, centred):
            nc.vector.tensor_tensor(df[:].indirect(picked[:, lo // 16 : hi // 16]), piece[:], weights[:, lo:hi], ALU.mult)

        last = slice(R - STORE, R)
        result_last = sb.tile([P, STORE], F32, name="result_last")
        nc.gpsimd.tensor_tensor(result_last[:], df[:, last], faded_last[:], ALU.add)
        nc.scalar.dma_start(out=out[:, last], in_=result_last[:])
        for lo in range(0, R - STORE, STORE):
            result = sb.tile([P, STORE], F32, name="result_%d" % lo)
            in_bank = slice(lo % BANK, lo % BANK + STORE)
            nc.vector.tensor_tensor(result[:], df[:, lo : lo + STORE], faded_halves[lo // BANK][:, in_bank], ALU.add)
            nc.sync.dma_start(out=out[:, lo : lo + STORE], in_=result[:])
